import numpy as np
CORES = [40,41,42,43,44,45,46,47,80,81,82,83,84,85,86,87]
N = 16
GROUPS = [[0,8],[1,9],[2,10],[3,11],[4,12],[5,13],[6,14],[7,15]]
def setup_inputs(rng):
    return {"x": rng.standard_normal((N, 128, 128), dtype=np.float32)}
def reference(x):
    y = np.empty((N, 128, 128), x.dtype)
    for g in GROUPS:
        s = x[g].min(axis=0)
        for r in g:
            y[r] = s
    return {"y": y}

from concourse.bass import DstId, RemoteDMATransfer

TILE = [128, 128]
SCRATCH = {
    "xs": ("dram", TILE, "float32"),
    "relay": ("dram", TILE, "float32"),
    "ina": ("dram", TILE, "float32"),
    "inb": ("dram", TILE, "float32"),
    "res": ("dram", TILE, "float32"),
}
SEMAPHORES = ["ld", "st", "handed", "got", "done", "sent"]

GATEWAYS = (2, 3, 6, 7)
OFF_CHIP, ON_CHIP = 8, 16
MIN = 3


def plan(T, topo):
    out = []
    for grp in T.tables["GROUPS"]:
        a, b = T.cores[grp[0]], T.cores[grp[1]]
        j = a % 8
        if j in GATEWAYS:
            fold, fwd = (topo.chip(a) ^ 1) * 8 + j, None
        else:
            fold, fwd = (topo.chip(b) ^ 1) * 8 + j + 2, topo.chip(b) * 8 + j + 2
        out.append((a, b, fold, fwd))
    return out


def rank_program(g, core, T, topo):
    sem = T.sem
    sent = [0]

    def send(dst_core, out_ap, in_ap, remote_sem):
        rid, pid, _ = topo.addr(dst_core)
        m = topo.mask(core, dst_core)
        g.remote_dma(out_ap, in_ap, remote_sem, sem.sent, pid, rid, m)
        sent[0] += OFF_CHIP if m == 0xFF else ON_CHIP

    pairs = plan(T, topo)

    for a, b, fold, fwd in pairs:
        if core == fold:
            g.wait_ge(sem.got, 2 * OFF_CHIP)
            ids = [DstId(rid=topo.addr(c)[0], pnc=topo.addr(c)[1]) for c in (a, b)]
            g.remote_dma_fused(
                [RemoteDMATransfer(dst_ids=ids, dma_engine_mask=0xFF, remote_sem=sem.done,
                                   srcs=[T.ina[:], T.inb[:]], dsts=[T.res[:], T.res[:]], alu_op=MIN)],
                local_sem=sem.sent)
            g.wait_ge(sem.sent, OFF_CHIP)
            return

    if T.rank_of(core) is None:
        return

    g.dma_start(T.xs[:], T.x[:]).then_inc(sem.ld, 16)
    g.wait_ge(sem.ld, 16)
    for a, b, fold, fwd in pairs:
        if core == a:
            send(fold, T.ina[:], T.xs[:], sem.got)
        elif core == b and fwd is None:
            send(fold, T.inb[:], T.xs[:], sem.got)
        elif core == b:
            send(fwd, T.relay[:], T.xs[:], sem.handed)
    for a, b, fold, fwd in pairs:
        if core == fwd:
            g.wait_ge(sem.handed, ON_CHIP)
            send(fold, T.inb[:], T.relay[:], sem.got)
    g.wait_ge(sem.done, OFF_CHIP)
    g.dma_start(T.y[:], T.res[:]).then_inc(sem.st, 16)
    g.wait_ge(sem.st, 16)
    g.wait_ge(sem.sent, sent[0])
